import numpy as np, ml_dtypes
CORES = [24,26,29,31,48,50,53,55]
N = 8
NH, QP = 4, 64
def setup_inputs(rng):
    return {"q": rng.standard_normal((N, 128, NH * QP), dtype=np.float32).astype(ml_dtypes.bfloat16), "k": rng.standard_normal((N, 128, NH * 128), dtype=np.float32).astype(ml_dtypes.bfloat16), "v": rng.standard_normal((N, 128, NH * 128), dtype=np.float32).astype(ml_dtypes.bfloat16)}
def setup_inputs_big(rng):
    d = setup_inputs(rng)
    for k in ("q", "k", "v"): d[k] = (d[k].astype(np.float32) * 1024.0).astype(d[k].dtype)
    return d
def setup_inputs_small(rng):
    d = setup_inputs(rng)
    for k in ("q", "k", "v"): d[k] = (d[k].astype(np.float32) * (1 / 1024.0)).astype(d[k].dtype)
    return d
def setup_inputs_apart(rng):
    d = setup_inputs(rng)
    f = (10.0 ** rng.permutation(np.linspace(-1.5, 1.5, N))).astype(np.float32).reshape(N, 1, 1)
    for k in ("q", "k", "v"): d[k] = (d[k].astype(np.float32) * f).astype(d[k].dtype)
    return d
def reference(q, k, v):
    Q, K, V = q.astype(np.float64), k.astype(np.float64), v.astype(np.float64)
    y = np.zeros((N, 128, NH * QP))
    for r in range(N):
        for h in range(NH):
            for j in range(N):
                S = np.maximum(K[j][:, 128 * h:128 * h + 128].T @ Q[r][:, QP * h:QP * h + QP], 0.0)
                y[r][:, QP * h:QP * h + QP] += V[j][:, 128 * h:128 * h + 128].T @ S
    return {"y": y.astype(ml_dtypes.bfloat16 if q.dtype != np.float64 else np.float64)}

@@ -1,0 +1,193 @@
+from concourse.bass import DstId, RemoteDMATransfer
+from concourse.mybir import AluOpType
+
+NH, QP, KP = 4, 64, 128
+NG = 2
+HG = NH // NG
+WQ, WK = HG * QP, HG * KP
+NJ = 4
+NCH = NJ * HG
+NSB = 4
+
+SCRATCH = {
+    "qs": ("sbuf", [128, NH * QP], "bfloat16"),
+    "kvs": ("sbuf", [128, NG, 2, WK], "bfloat16"),
+    "Qf": ("sbuf", [128, 2 * WQ], "bfloat16"),
+    "Qr": ("sbuf", [128, NJ * WQ], "bfloat16"),
+    "Qg": ("sbuf", [128, NJ * WQ], "bfloat16"),
+    "KVg": ("sbuf", [128, NJ, 2, WK], "bfloat16"),
+    "zero": ("sbuf", [128, NJ * QP], "bfloat16"),
+    "Sb": ("sbuf", [128, NCH, NJ * QP], "bfloat16"),
+    "Ob": ("sbuf", [128, NJ * WQ], "bfloat16"),
+    "Orm": ("sbuf", [128, NH * QP], "bfloat16"),
+    "Olc": ("sbuf", [128, NH * QP], "bfloat16"),
+    "yb": ("sbuf", [128, NH * QP], "bfloat16"),
+}
+for _i in range(NSB):
+    SCRATCH["Sp%d" % _i] = ("psum", [128, 512], "float32")
+for _i in range(NJ):
+    SCRATCH["Op%d" % _i] = ("psum", [128, 512], "float32")
+
+SEMAPHORES = ["ld_q", "ld_k", "ld_v", "ld_qo", "sent", "qf", "qr1", "qr2", "ql", "kv", "orm", "olc", "zs", "sadd", "st"]
+SEMAPHORES += ["sS%d" % _i for _i in range(NCH)] + ["sR%d" % _i for _i in range(NCH)]
+SEMAPHORES += ["sO%d" % _i for _i in range(NCH)] + ["sC%d" % _i for _i in range(NJ)]
+
+
+def _bits(m):
+    return [e for e in range(m.bit_length()) if (m >> e) & 1]
+
+
+def _roles(T, topo):
+    chips = sorted(set(topo.chip(c) for c in T.cores))
+    on = dict((ch, [c for c in T.cores if topo.chip(c) == ch]) for ch in chips)
+    out = {}
+    for ch in chips:
+        far = [c for o in chips if o != ch for c in on[o]]
+        port = sorted([c for c in on[ch] if all(topo.may_write(c, d) for d in far)], key=topo.die)
+        rest = sorted([c for c in on[ch] if c not in port], key=topo.die)
+        out[ch] = (on[ch], port, rest)
+    return out
+
+
+def rank_program(g, core, T, topo):
+    if T.rank_of(core) is None:
+        return
+    te, ve, sy, sc = g.tensor, g.vector, g.sync, g.scalar
+    sem = T.sem
+    roles = _roles(T, topo)
+    here = topo.chip(core)
+    there = [ch for ch in roles if ch != here][0]
+    ranks, P, L = roles[here]
+    _fr, fP, fL = roles[there]
+    me = ranks.index(core)
+    is_port = core in P
+    grp = P.index(core) if is_port else L.index(core)
+    nsent = [0]
+
+    def send(items):
+        used, trs = 0, []
+        for dst, dap, sap, n, rs in sorted(items, key=lambda it: len(_bits(topo.mask(core, it[0])))):
+            m = sum(1 << e for e in [e for e in _bits(topo.mask(core, dst)) if not (used >> e) & 1][:n])
+            used |= m
+            nsent[0] += n
+            trs.append((dst, dap, sap, m, rs))
+        if len(trs) == 1:
+            dst, dap, sap, m, rs = trs[0]
+            rid, pid, _se = topo.addr(dst)
+            g.remote_dma(out_ap=dap, in_ap=sap, remote_sem=rs, local_sem=sem.sent, pid=pid, routing_id=rid,
+                         dma_engine_mask=m)
+            return
+        lst = []
+        for dst, dap, sap, m, rs in trs:
+            rid, pid, _se = topo.addr(dst)
+            lst.append(RemoteDMATransfer(dst_ids=[DstId(rid=rid, pnc=pid)], dma_engine_mask=m, remote_sem=rs,
+                                         src=sap, dst=dap))
+        g.remote_dma_fused(lst, local_sem=sem.sent)
+
+    def qcols(t, s):
+        return t[:, s * WQ:(s + 1) * WQ]
+
+    sy.dma_start(T.qs[:, :], T.q[:, :]).then_inc(sem.ld_q, 16)
+    if not is_port:
+        sc.dma_start(qcols(T.Qg, me), qcols(T.q, grp)).then_inc(sem.ld_qo, 16)
+    sy.dma_start(T.kvs[:, :, 0, :], T.k[:, :]).then_inc(sem.ld_k, 16)
+    sc.dma_start(T.kvs[:, :, 1, :], T.v[:, :]).then_inc(sem.ld_v, 16)
+
+    g.wait_ge(sem.ld_q, 16)
+    items = []
+    for a in range(NG):
+        if is_port:
+            items.append((fP[a], qcols(T.Qr, grp), qcols(T.qs, a), 4, sem.qr1))
+            items.append((L[a], qcols(T.Qg, me), qcols(T.qs, a), 2, sem.ql))
+        else:
+            items.append((P[a], qcols(T.Qf, grp), qcols(T.qs, a), 4, sem.qf))
+            if L[a] != core:
+                items.append((L[a], qcols(T.Qg, me), qcols(T.qs, a), 2, sem.ql))
+    send(items)
+
+    g.wait_ge(sem.ld_k, 16)
+    g.wait_ge(sem.ld_v, 16)
+    for group in (P, L):
+        dsts = [(a, d) for a, d in enumerate(group) if d != core]
+        send([(d, T.KVg[:, me], T.kvs[:, a], 16 // len(dsts), sem.kv) for a, d in dsts])
+
+    if is_port:
+        g.wait_ge(sem.qf, 8)
+        send([(fP[grp], T.Qr[:, 2 * WQ:4 * WQ], T.Qf[:, :], 8, sem.qr2)])
+
+    if is_port:
+        Q, slot, served = T.Qr, list(range(NJ)), fP + fL
+        phases = [(list(range(0, NCH // 2)), [(sem.qr1, 8)]), (list(range(NCH // 2, NCH)), [(sem.qr2, 8)])]
+    else:
+        slot = [i for i in range(NJ) if i != me] + [me]
+        Q, served = T.Qg, [ranks[i] for i in slot]
+        phases = [(list(range(NCH)), [(sem.ql, 6), (sem.ld_qo, 16)])]
+
+    def kvp(j, w, hh):
+        t = T.kvs[:, grp, w, hh * KP:(hh + 1) * KP] if j == me else T.KVg[:, j, w, hh * KP:(hh + 1) * KP]
+        return t
+
+    def mm_s(c):
+        pos, hh = divmod(c, HG)
+        col = slot[pos] * WQ + hh * QP
+        for j in range(NJ):
+            te.matmul(T["Sp%d" % (c % NSB)][:, j * QP:(j + 1) * QP], kvp(j, 0, hh), Q[:, col:col + QP],
+                      start=True, stop=True).then_inc(sem["sS%d" % c], 1)
+
+    def mm_o(c):
+        pos, hh = divmod(c, HG)
+        te.wait_ge(sem["sR%d" % c], 1)
+        for j in range(NJ):
+            te.matmul(T["Op%d" % pos][:, hh * QP:(hh + 1) * QP], kvp(j, 1, hh), T.Sb[:, c, j * QP:(j + 1) * QP],
+                      start=(j == 0), stop=(j == NJ - 1)).then_inc(sem["sO%d" % c], 1)
+
+    def relu(c):
+        ve.wait_ge(sem["sS%d" % c], NJ)
+        ve.tensor_tensor(T.Sb[:, c, :], T["Sp%d" % (c % NSB)][:, 0:NJ * QP], T.zero[:, :],
+                         AluOpType.max).then_inc(sem["sR%d" % c], 1)
+
+    def finish(pos):
+        for hh in range(HG):
+            ve.wait_ge(sem["sO%d" % (pos * HG + hh)], NJ)
+        out = qcols(T.Olc, grp) if served[pos] == core else qcols(T.Ob, pos)
+        ve.tensor_copy(out, T["Op%d" % pos][:, 0:WQ]).then_inc(sem["sC%d" % pos], 1)
+
+    te.wait_ge(sem.ld_k, 16)
+    te.wait_ge(sem.ld_v, 16)
+    te.wait_ge(sem.kv, 32)
+    for chunks, waits in phases:
+        for s, n in waits:
+            te.wait_ge(s, n)
+        for i, c in enumerate(chunks):
+            mm_s(c)
+            if i > 0:
+                mm_o(chunks[i - 1])
+        mm_o(chunks[-1])
+
+    ve.memset(T.zero[:, :], 0.0).then_inc(sem.zs, 1)
+    ve.wait_ge(sem.zs, 1)
+    for chunks, waits in phases:
+        for i, c in enumerate(chunks):
+            relu(c)
+            if i > 0 and chunks[i - 1] % HG == HG - 1:
+                finish(chunks[i - 1] // HG)
+        finish(chunks[-1] // HG)
+
+    for pos in range(NJ):
+        if served[pos] == core:
+            continue
+        g.wait_ge(sem["sC%d" % pos], 1)
+        if is_port:
+            send([(served[pos], qcols(T.Orm, grp), qcols(T.Ob, pos), 8, sem.orm)])
+        else:
+            send([(served[pos], qcols(T.Olc, grp), qcols(T.Ob, pos), 16, sem.olc)])
+
+    if not is_port:
+        ve.wait_ge(sem["sC%d" % (NJ - 1)], 1)
+    ve.wait_ge(sem.olc, 16 * len([d for d in L if d != core]))
+    ve.wait_ge(sem.orm, 8 * NG)
+    ve.tensor_tensor(T.yb[:, :], T.Orm[:, :], T.Olc[:, :], AluOpType.add).then_inc(sem.sadd, 1)
+    sy.wait_ge(sem.sadd, 1)
+    sy.dma_start(T.y[:, :], T.yb[:, :]).then_inc(sem.st, 16)
+    sy.wait_ge(sem.st, 16)
+    g.wait_ge(sem.sent, nsent[0])

@@ -2,35 +2,32 @@ from concourse.bass import DstId, RemoteDMATransfer
 from concourse.mybir import AluOpType
 
 NH, QP, KP = 4, 64, 128
-NG = 2
-HG = NH // NG
-WQ, WK = HG * QP, HG * KP
 NJ = 4
-NCH = NJ * HG
-NSB = 4
+WP = 2 * KP
+NO = 8
 
 SCRATCH = {
     "qs": ("sbuf", [128, NH * QP], "bfloat16"),
-    "kvs": ("sbuf", [128, NG, 2, WK], "bfloat16"),
-    "Qf": ("sbuf", [128, 2 * WQ], "bfloat16"),
-    "Qr": ("sbuf", [128, NJ * WQ], "bfloat16"),
-    "Qg": ("sbuf", [128, NJ * WQ], "bfloat16"),
-    "KVg": ("sbuf", [128, NJ, 2, WK], "bfloat16"),
+    "kvs": ("sbuf", [128, NH * WP], "bfloat16"),
+    "Qf": ("sbuf", [128, 2, 2 * QP], "bfloat16"),
+    "Qr": ("sbuf", [128, NJ * QP], "bfloat16"),
+    "Qg": ("sbuf", [128, NJ * QP], "bfloat16"),
+    "KVg": ("sbuf", [128, NJ, WP], "bfloat16"),
     "zero": ("sbuf", [128, NJ * QP], "bfloat16"),
-    "Sb": ("sbuf", [128, NCH, NJ * QP], "bfloat16"),
-    "Ob": ("sbuf", [128, NJ * WQ], "bfloat16"),
+    "Sb": ("sbuf", [128, NJ, NJ * QP], "bfloat16"),
+    "Ob": ("sbuf", [128, NJ * QP], "bfloat16"),
     "Orm": ("sbuf", [128, NH * QP], "bfloat16"),
     "Olc": ("sbuf", [128, NH * QP], "bfloat16"),
     "yb": ("sbuf", [128, NH * QP], "bfloat16"),
 }
-for _i in range(NSB):
-    SCRATCH["Sp%d" % _i] = ("psum", [128, 512], "float32")
 for _i in range(NJ):
+    SCRATCH["Sp%d" % _i] = ("psum", [128, 512], "float32")
     SCRATCH["Op%d" % _i] = ("psum", [128, 512], "float32")
 
-SEMAPHORES = ["ld_q", "ld_k", "ld_v", "ld_qo", "sent", "qf", "qr1", "qr2", "ql", "kv", "orm", "olc", "zs", "sadd", "st"]
-SEMAPHORES += ["sS%d" % _i for _i in range(NCH)] + ["sR%d" % _i for _i in range(NCH)]
-SEMAPHORES += ["sO%d" % _i for _i in range(NCH)] + ["sC%d" % _i for _i in range(NJ)]
+SEMAPHORES = ["ld_q", "ldA", "ldB", "sent", "qf", "qr1", "qr2", "ql", "kv", "zs", "sadd", "st"]
+SEMAPHORES += ["oh%d" % _i for _i in range(NH)]
+for _n in ("sS", "sR", "sO", "sC"):
+    SEMAPHORES += [_n + "%d" % _i for _i in range(NJ)]
 
 
 def _bits(m):
@@ -43,118 +40,133 @@ def _roles(T, topo):
     out = {}
     for ch in chips:
         far = [c for o in chips if o != ch for c in on[o]]
-        port = sorted([c for c in on[ch] if all(topo.may_write(c, d) for d in far)], key=topo.die)
-        rest = sorted([c for c in on[ch] if c not in port], key=topo.die)
+        allc = [c for c in range(topo.CORES_PER_CHIP * topo.CHIPS) if topo.chip(c) == ch]
+        port = sorted([c for c in allc if all(topo.may_write(c, d) for d in far)], key=lambda c: (topo.die(c), c))
+        rest = sorted([c for c in allc if c not in port], key=lambda c: (topo.die(c), c))
         out[ch] = (on[ch], port, rest)
     return out
 
 
 def rank_program(g, core, T, topo):
-    if T.rank_of(core) is None:
+    roles = _roles(T, topo)
+    here = topo.chip(core)
+    if here not in roles:
         return
     te, ve, sy, sc = g.tensor, g.vector, g.sync, g.scalar
     sem = T.sem
-    roles = _roles(T, topo)
-    here = topo.chip(core)
     there = [ch for ch in roles if ch != here][0]
     ranks, P, L = roles[here]
-    _fr, fP, fL = roles[there]
-    me = ranks.index(core)
+    franks, fP, fL = roles[there]
+    PR, LR = [c for c in P if c in ranks], [c for c in L if c in ranks]
+    RL = [c for c in P if c not in ranks]
+    fPR, fLR = [c for c in fP if c in franks], [c for c in fL if c in franks]
+    HR = NH // len(RL)
+    is_rank = core in ranks
+    me = ranks.index(core) if is_rank else None
     is_port = core in P
     grp = P.index(core) if is_port else L.index(core)
     nsent = [0]
 
+    OFF = _bits(topo.mask(core, fP[0]))
+    ENG = OFF + [e for e in _bits(topo.mask(core, [c for c in P + L if c != core][0])) if e not in OFF]
+
+    def eg(i, n):
+        return ENG[i * n:(i + 1) * n]
+
     def send(items):
-        used, trs = 0, []
-        for dst, dap, sap, n, rs in sorted(items, key=lambda it: len(_bits(topo.mask(core, it[0])))):
-            m = sum(1 << e for e in [e for e in _bits(topo.mask(core, dst)) if not (used >> e) & 1][:n])
-            used |= m
-            nsent[0] += n
-            trs.append((dst, dap, sap, m, rs))
-        if len(trs) == 1:
-            dst, dap, sap, m, rs = trs[0]
-            rid, pid, _se = topo.addr(dst)
-            g.remote_dma(out_ap=dap, in_ap=sap, remote_sem=rs, local_sem=sem.sent, pid=pid, routing_id=rid,
-                         dma_engine_mask=m)
-            return
         lst = []
-        for dst, dap, sap, m, rs in trs:
+        for dst, dap, sap, engs, rs in items:
             rid, pid, _se = topo.addr(dst)
+            m = sum(1 << e for e in engs)
+            nsent[0] += len(engs)
+            if len(items) == 1:
+                g.remote_dma(out_ap=dap, in_ap=sap, remote_sem=rs, local_sem=sem.sent, pid=pid, routing_id=rid,
+                             dma_engine_mask=m)
+                return
             lst.append(RemoteDMATransfer(dst_ids=[DstId(rid=rid, pnc=pid)], dma_engine_mask=m, remote_sem=rs,
                                          src=sap, dst=dap))
         g.remote_dma_fused(lst, local_sem=sem.sent)
 
-    def qcols(t, s):
-        return t[:, s * WQ:(s + 1) * WQ]
+    def qcol(t, s):
+        return t[:, s * QP:(s + 1) * QP]
 
-    sy.dma_start(T.qs[:, :], T.q[:, :]).then_inc(sem.ld_q, 16)
-    if not is_port:
-        sc.dma_start(qcols(T.Qg, me), qcols(T.q, grp)).then_inc(sem.ld_qo, 16)
-    sy.dma_start(T.kvs[:, :, 0, :], T.k[:, :]).then_inc(sem.ld_k, 16)
-    sc.dma_start(T.kvs[:, :, 1, :], T.v[:, :]).then_inc(sem.ld_v, 16)
+    if is_rank:
+        sy.dma_start(T.qs[:, :], T.q[:, :]).then_inc(sem.ld_q, 16)
+        sc.dma_start(T.kvs[:, 0:KP], T.v[:, 0:KP]).then_inc(sem.ldA, 16)
+        sy.dma_start(T.kvs[:, KP:3 * KP], T.k[:, 0:2 * KP]).then_inc(sem.ldA, 16)
+        sc.dma_start(T.kvs[:, 3 * KP:5 * KP], T.v[:, KP:3 * KP]).then_inc(sem.ldA, 16)
+        sy.dma_start(T.kvs[:, 5 * KP:7 * KP], T.k[:, 2 * KP:4 * KP]).then_inc(sem.ldB, 16)
+        sc.dma_start(T.kvs[:, 7 * KP:8 * KP], T.v[:, 3 * KP:4 * KP]).then_inc(sem.ldB, 16)
 
-    g.wait_ge(sem.ld_q, 16)
-    items = []
-    for a in range(NG):
+        g.wait_ge(sem.ld_q, 16)
         if is_port:
-            items.append((fP[a], qcols(T.Qr, grp), qcols(T.qs, a), 4, sem.qr1))
-            items.append((L[a], qcols(T.Qg, me), qcols(T.qs, a), 2, sem.ql))
+            items = [(fP[a], qcol(T.Qr, PR.index(core)), qcol(T.qs, a), eg(a, 2), sem.qr1) for a in range(NH)]
+            items += [(L[a], qcol(T.Qg, me), qcol(T.qs, a), eg(NH + a, 2), sem.ql) for a in range(NH)]
+            send(items)
         else:
-            items.append((P[a], qcols(T.Qf, grp), qcols(T.qs, a), 4, sem.qf))
-            if L[a] != core:
-                items.append((L[a], qcols(T.Qg, me), qcols(T.qs, a), 2, sem.ql))
-    send(items)
+            i = LR.index(core)
+            send([(RL[a // HR], T.Qf[:, a % HR, i * QP:(i + 1) * QP], qcol(T.qs, a), eg(a, 4), sem.qf)
+                  for a in range(NH)])
+            send([(L[a], qcol(T.Qg, me), qcol(T.qs, a), eg(n, 4), sem.ql)
+                  for n, a in enumerate([a for a in range(NH) if L[a] != core])])
 
-    g.wait_ge(sem.ld_k, 16)
-    g.wait_ge(sem.ld_v, 16)
-    for group in (P, L):
-        dsts = [(a, d) for a, d in enumerate(group) if d != core]
-        send([(d, T.KVg[:, me], T.kvs[:, a], 16 // len(dsts), sem.kv) for a, d in dsts])
+        for half, (s, n) in enumerate(((sem.ldA, 48), (sem.ldB, 32))):
+            g.wait_ge(s, n)
+            dsts = [(a, d) for a in (2 * half, 2 * half + 1) for d in (P[a], L[a]) if d != core]
+            send([(d, T.KVg[:, me], T.kvs[:, a * WP:(a + 1) * WP], eg(3 - x, 4), sem.kv)
+                  for x, (a, d) in enumerate(dsts)])
+
+    if core in RL:
+        r = RL.index(core)
+        g.wait_ge(sem.qf, len(LR) * HR * 4)
+        send([(fP[r * HR + hh], T.Qr[:, len(PR) * QP:NJ * QP], T.Qf[:, hh, :], eg(hh, 4), sem.qr2)
+              for hh in range(HR)])
 
     if is_port:
-        g.wait_ge(sem.qf, 8)
-        send([(fP[grp], T.Qr[:, 2 * WQ:4 * WQ], T.Qf[:, :], 8, sem.qr2)])
-
-    if is_port:
-        Q, slot, served = T.Qr, list(range(NJ)), fP + fL
-        phases = [(list(range(0, NCH // 2)), [(sem.qr1, 8)]), (list(range(NCH // 2, NCH)), [(sem.qr2, 8)])]
+        Q, slot, served = T.Qr, list(range(NJ)), fPR + fLR
+        np_ = len(fPR)
+        phases = [(list(range(0, np_)), [(sem.qr1, 2 * np_)]), (list(range(np_, NJ)), [(sem.qr2, 4)])]
     else:
-        slot = [i for i in range(NJ) if i != me] + [me]
+        slot = [i for i in range(NJ) if i != me] + ([me] if is_rank else [])
         Q, served = T.Qg, [ranks[i] for i in slot]
-        phases = [(list(range(NCH)), [(sem.ql, 6), (sem.ld_qo, 16)])]
+        waits = [(sem.ql, 2 * len(PR) + 4 * len([c for c in LR if c != core]))]
+        if is_rank:
+            waits.append((sem.ld_q, 16))
+        phases = [(list(range(NJ)), waits)]
+    koff = KP if grp % 2 == 0 else 0
 
-    def kvp(j, w, hh):
-        t = T.kvs[:, grp, w, hh * KP:(hh + 1) * KP] if j == me else T.KVg[:, j, w, hh * KP:(hh + 1) * KP]
-        return t
+    def kvp(j, w):
+        o = koff if w == 0 else KP - koff
+        if j == me:
+            return T.kvs[:, grp * WP + o:grp * WP + o + KP]
+        return T.KVg[:, j, o:o + KP]
 
     def mm_s(c):
-        pos, hh = divmod(c, HG)
-        col = slot[pos] * WQ + hh * QP
+        rhs = qcol(T.qs, grp) if served[c] == core else qcol(Q, slot[c])
         for j in range(NJ):
-            te.matmul(T["Sp%d" % (c % NSB)][:, j * QP:(j + 1) * QP], kvp(j, 0, hh), Q[:, col:col + QP],
+            te.matmul(T["Sp%d" % c][:, j * QP:(j + 1) * QP], kvp(j, 0), rhs,
                       start=True, stop=True).then_inc(sem["sS%d" % c], 1)
 
     def mm_o(c):
-        pos, hh = divmod(c, HG)
         te.wait_ge(sem["sR%d" % c], 1)
         for j in range(NJ):
-            te.matmul(T["Op%d" % pos][:, hh * QP:(hh + 1) * QP], kvp(j, 1, hh), T.Sb[:, c, j * QP:(j + 1) * QP],
+            te.matmul(T["Op%d" % c][:, 0:QP], kvp(j, 1), T.Sb[:, c, j * QP:(j + 1) * QP],
                       start=(j == 0), stop=(j == NJ - 1)).then_inc(sem["sO%d" % c], 1)
 
     def relu(c):
         ve.wait_ge(sem["sS%d" % c], NJ)
-        ve.tensor_tensor(T.Sb[:, c, :], T["Sp%d" % (c % NSB)][:, 0:NJ * QP], T.zero[:, :],
+        ve.tensor_tensor(T.Sb[:, c, :], T["Sp%d" % c][:, 0:NJ * QP], T.zero[:, :],
                          AluOpType.max).then_inc(sem["sR%d" % c], 1)
 
-    def finish(pos):
-        for hh in range(HG):
-            ve.wait_ge(sem["sO%d" % (pos * HG + hh)], NJ)
-        out = qcols(T.Olc, grp) if served[pos] == core else qcols(T.Ob, pos)
-        ve.tensor_copy(out, T["Op%d" % pos][:, 0:WQ]).then_inc(sem["sC%d" % pos], 1)
+    def finish(c):
+        ve.wait_ge(sem["sO%d" % c], NJ)
+        out = qcol(T.Olc, grp) if served[c] == core else qcol(T.Ob, c)
+        ve.tensor_copy(out, T["Op%d" % c][:, 0:QP]).then_inc(sem["sC%d" % c], 1)
 
-    te.wait_ge(sem.ld_k, 16)
-    te.wait_ge(sem.ld_v, 16)
-    te.wait_ge(sem.kv, 32)
+    if is_rank:
+        te.wait_ge(sem.ldA, 48)
+        te.wait_ge(sem.ldB, 32)
+    te.wait_ge(sem.kv, 4 * len([c for c in ranks if c != core]))
     for chunks, waits in phases:
         for s, n in waits:
             te.wait_ge(s, n)
@@ -169,25 +181,23 @@ def rank_program(g, core, T, topo):
     for chunks, waits in phases:
         for i, c in enumerate(chunks):
             relu(c)
-            if i > 0 and chunks[i - 1] % HG == HG - 1:
-                finish(chunks[i - 1] // HG)
-        finish(chunks[-1] // HG)
+            if i > 0:
+                finish(chunks[i - 1])
+        finish(chunks[-1])
 
-    for pos in range(NJ):
-        if served[pos] == core:
+    for c in range(NJ):
+        if served[c] == core:
             continue
-        g.wait_ge(sem["sC%d" % pos], 1)
-        if is_port:
-            send([(served[pos], qcols(T.Orm, grp), qcols(T.Ob, pos), 8, sem.orm)])
-        else:
-            send([(served[pos], qcols(T.Olc, grp), qcols(T.Ob, pos), 16, sem.olc)])
+        g.wait_ge(sem["sC%d" % c], 1)
+        send([(served[c], qcol(T.Orm if is_port else T.Olc, grp), qcol(T.Ob, c), eg(0, NO), sem["oh%d" % grp])])
 
-    if not is_port:
-        ve.wait_ge(sem["sC%d" % (NJ - 1)], 1)
-    ve.wait_ge(sem.olc, 16 * len([d for d in L if d != core]))
-    ve.wait_ge(sem.orm, 8 * NG)
-    ve.tensor_tensor(T.yb[:, :], T.Orm[:, :], T.Olc[:, :], AluOpType.add).then_inc(sem.sadd, 1)
-    sy.wait_ge(sem.sadd, 1)
-    sy.dma_start(T.y[:, :], T.yb[:, :]).then_inc(sem.st, 16)
-    sy.wait_ge(sem.st, 16)
+    if is_rank:
+        for a in range(NH):
+            if L[a] == core:
+                ve.wait_ge(sem["sC%d" % (NJ - 1)], 1)
+            ve.wait_ge(sem["oh%d" % a], NO + (NO if L[a] != core else 0))
+            ve.tensor_tensor(qcol(T.yb, a), qcol(T.Orm, a), qcol(T.Olc, a), AluOpType.add).then_inc(sem.sadd, 1)
+        sy.wait_ge(sem.sadd, NH)
+        sy.dma_start(T.y[:, :], T.yb[:, :]).then_inc(sem.st, 16)
+        sy.wait_ge(sem.st, 16)
     g.wait_ge(sem.sent, nsent[0])

from concourse.bass import DstId, RemoteDMATransfer
from concourse.mybir import AluOpType

NH, QP, KP = 4, 64, 128
NJ = 4
WP = 2 * KP
NO = 8

SCRATCH = {
    "qs": ("sbuf", [128, NH * QP], "bfloat16"),
    "kvs": ("sbuf", [128, NH * WP], "bfloat16"),
    "Qf": ("sbuf", [128, 2, 2 * QP], "bfloat16"),
    "Qr": ("sbuf", [128, NJ * QP], "bfloat16"),
    "Qg": ("sbuf", [128, NJ * QP], "bfloat16"),
    "KVg": ("sbuf", [128, NJ, WP], "bfloat16"),
    "zero": ("sbuf", [128, NJ * QP], "bfloat16"),
    "Sb": ("sbuf", [128, NJ, NJ * QP], "bfloat16"),
    "Ob": ("sbuf", [128, NJ * QP], "bfloat16"),
    "Orm": ("sbuf", [128, NH * QP], "bfloat16"),
    "Olc": ("sbuf", [128, NH * QP], "bfloat16"),
    "yb": ("sbuf", [128, NH * QP], "bfloat16"),
}
for _i in range(NJ):
    SCRATCH["Sp%d" % _i] = ("psum", [128, 512], "float32")
    SCRATCH["Op%d" % _i] = ("psum", [128, 512], "float32")

SEMAPHORES = ["ld_q", "ldA", "ldB", "sent", "qf", "qr1", "qr2", "ql", "kv", "zs", "sadd", "st"]
SEMAPHORES += ["oh%d" % _i for _i in range(NH)]
for _n in ("sS", "sR", "sO", "sC"):
    SEMAPHORES += [_n + "%d" % _i for _i in range(NJ)]


def _bits(m):
    return [e for e in range(m.bit_length()) if (m >> e) & 1]


def _roles(T, topo):
    chips = sorted(set(topo.chip(c) for c in T.cores))
    on = dict((ch, [c for c in T.cores if topo.chip(c) == ch]) for ch in chips)
    out = {}
    for ch in chips:
        far = [c for o in chips if o != ch for c in on[o]]
        allc = [c for c in range(topo.CORES_PER_CHIP * topo.CHIPS) if topo.chip(c) == ch]
        port = sorted([c for c in allc if all(topo.may_write(c, d) for d in far)], key=lambda c: (topo.die(c), c))
        rest = sorted([c for c in allc if c not in port], key=lambda c: (topo.die(c), c))
        out[ch] = (on[ch], port, rest)
    return out


def rank_program(g, core, T, topo):
    roles = _roles(T, topo)
    here = topo.chip(core)
    if here not in roles:
        return
    te, ve, sy, sc = g.tensor, g.vector, g.sync, g.scalar
    sem = T.sem
    there = [ch for ch in roles if ch != here][0]
    ranks, P, L = roles[here]
    franks, fP, fL = roles[there]
    PR, LR = [c for c in P if c in ranks], [c for c in L if c in ranks]
    RL = [c for c in P if c not in ranks]
    fPR, fLR = [c for c in fP if c in franks], [c for c in fL if c in franks]
    HR = NH // len(RL)
    is_rank = core in ranks
    me = ranks.index(core) if is_rank else None
    is_port = core in P
    grp = P.index(core) if is_port else L.index(core)
    nsent = [0]

    OFF = _bits(topo.mask(core, fP[0]))
    ENG = OFF + [e for e in _bits(topo.mask(core, [c for c in P + L if c != core][0])) if e not in OFF]

    def eg(i, n):
        return ENG[i * n:(i + 1) * n]

    def send(items):
        lst = []
        for dst, dap, sap, engs, rs in items:
            rid, pid, _se = topo.addr(dst)
            m = sum(1 << e for e in engs)
            nsent[0] += len(engs)
            if len(items) == 1:
                g.remote_dma(out_ap=dap, in_ap=sap, remote_sem=rs, local_sem=sem.sent, pid=pid, routing_id=rid,
                             dma_engine_mask=m)
                return
            lst.append(RemoteDMATransfer(dst_ids=[DstId(rid=rid, pnc=pid)], dma_engine_mask=m, remote_sem=rs,
                                         src=sap, dst=dap))
        g.remote_dma_fused(lst, local_sem=sem.sent)

    def qcol(t, s):
        return t[:, s * QP:(s + 1) * QP]

    if is_rank:
        sy.dma_start(T.qs[:, :], T.q[:, :]).then_inc(sem.ld_q, 16)
        sc.dma_start(T.kvs[:, 0:KP], T.v[:, 0:KP]).then_inc(sem.ldA, 16)
        sy.dma_start(T.kvs[:, KP:3 * KP], T.k[:, 0:2 * KP]).then_inc(sem.ldA, 16)
        sc.dma_start(T.kvs[:, 3 * KP:5 * KP], T.v[:, KP:3 * KP]).then_inc(sem.ldA, 16)
        sy.dma_start(T.kvs[:, 5 * KP:7 * KP], T.k[:, 2 * KP:4 * KP]).then_inc(sem.ldB, 16)
        sc.dma_start(T.kvs[:, 7 * KP:8 * KP], T.v[:, 3 * KP:4 * KP]).then_inc(sem.ldB, 16)

        g.wait_ge(sem.ld_q, 16)
        if is_port:
            items = [(fP[a], qcol(T.Qr, PR.index(core)), qcol(T.qs, a), eg(a, 2), sem.qr1) for a in range(NH)]
            items += [(L[a], qcol(T.Qg, me), qcol(T.qs, a), eg(NH + a, 2), sem.ql) for a in range(NH)]
            send(items)
        else:
            i = LR.index(core)
            send([(RL[a // HR], T.Qf[:, a % HR, i * QP:(i + 1) * QP], qcol(T.qs, a), eg(a, 4), sem.qf)
                  for a in range(NH)])
            send([(L[a], qcol(T.Qg, me), qcol(T.qs, a), eg(n, 4), sem.ql)
                  for n, a in enumerate([a for a in range(NH) if L[a] != core])])

        for half, (s, n) in enumerate(((sem.ldA, 48), (sem.ldB, 32))):
            g.wait_ge(s, n)
            dsts = [(a, d) for a in (2 * half, 2 * half + 1) for d in (P[a], L[a]) if d != core]
            send([(d, T.KVg[:, me], T.kvs[:, a * WP:(a + 1) * WP], eg(3 - x, 4), sem.kv)
                  for x, (a, d) in enumerate(dsts)])

    if core in RL:
        r = RL.index(core)
        g.wait_ge(sem.qf, len(LR) * HR * 4)
        send([(fP[r * HR + hh], T.Qr[:, len(PR) * QP:NJ * QP], T.Qf[:, hh, :], eg(hh, 4), sem.qr2)
              for hh in range(HR)])

    if is_port:
        Q, slot, served = T.Qr, list(range(NJ)), fPR + fLR
        np_ = len(fPR)
        phases = [(list(range(0, np_)), [(sem.qr1, 2 * np_)]), (list(range(np_, NJ)), [(sem.qr2, 4)])]
    else:
        slot = [i for i in range(NJ) if i != me] + ([me] if is_rank else [])
        Q, served = T.Qg, [ranks[i] for i in slot]
        waits = [(sem.ql, 2 * len(PR) + 4 * len([c for c in LR if c != core]))]
        if is_rank:
            waits.append((sem.ld_q, 16))
        phases = [(list(range(NJ)), waits)]
    koff = KP if grp % 2 == 0 else 0

    def kvp(j, w):
        o = koff if w == 0 else KP - koff
        if j == me:
            return T.kvs[:, grp * WP + o:grp * WP + o + KP]
        return T.KVg[:, j, o:o + KP]

    def mm_s(c):
        rhs = qcol(T.qs, grp) if served[c] == core else qcol(Q, slot[c])
        for j in range(NJ):
            te.matmul(T["Sp%d" % c][:, j * QP:(j + 1) * QP], kvp(j, 0), rhs,
                      start=True, stop=True).then_inc(sem["sS%d" % c], 1)

    def mm_o(c):
        te.wait_ge(sem["sR%d" % c], 1)
        for j in range(NJ):
            te.matmul(T["Op%d" % c][:, 0:QP], kvp(j, 1), T.Sb[:, c, j * QP:(j + 1) * QP],
                      start=(j == 0), stop=(j == NJ - 1)).then_inc(sem["sO%d" % c], 1)

    def relu(c):
        ve.wait_ge(sem["sS%d" % c], NJ)
        ve.tensor_tensor(T.Sb[:, c, :], T["Sp%d" % c][:, 0:NJ * QP], T.zero[:, :],
                         AluOpType.max).then_inc(sem["sR%d" % c], 1)

    def finish(c):
        ve.wait_ge(sem["sO%d" % c], NJ)
        out = qcol(T.Olc, grp) if served[c] == core else qcol(T.Ob, c)
        ve.tensor_copy(out, T["Op%d" % c][:, 0:QP]).then_inc(sem["sC%d" % c], 1)

    if is_rank:
        te.wait_ge(sem.ldA, 48)
        te.wait_ge(sem.ldB, 32)
    te.wait_ge(sem.kv, 4 * len([c for c in ranks if c != core]))
    for chunks, waits in phases:
        for s, n in waits:
            te.wait_ge(s, n)
        for i, c in enumerate(chunks):
            mm_s(c)
            if i > 0:
                mm_o(chunks[i - 1])
        mm_o(chunks[-1])

    ve.memset(T.zero[:, :], 0.0).then_inc(sem.zs, 1)
    ve.wait_ge(sem.zs, 1)
    for chunks, waits in phases:
        for i, c in enumerate(chunks):
            relu(c)
            if i > 0:
                finish(chunks[i - 1])
        finish(chunks[-1])

    for c in range(NJ):
        if served[c] == core:
            continue
        g.wait_ge(sem["sC%d" % c], 1)
        send([(served[c], qcol(T.Orm if is_port else T.Olc, grp), qcol(T.Ob, c), eg(0, NO), sem["oh%d" % grp])])

    if is_rank:
        for a in range(NH):
            if L[a] == core:
                ve.wait_ge(sem["sC%d" % (NJ - 1)], 1)
            ve.wait_ge(sem["oh%d" % a], NO + (NO if L[a] != core else 0))
            ve.tensor_tensor(qcol(T.yb, a), qcol(T.Orm, a), qcol(T.Olc, a), AluOpType.add).then_inc(sem.sadd, 1)
        sy.wait_ge(sem.sadd, NH)
        sy.dma_start(T.y[:, :], T.yb[:, :]).then_inc(sem.st, 16)
        sy.wait_ge(sem.st, 16)
    g.wait_ge(sem.sent, nsent[0])
